import numpy as np
import ml_dtypes


def mxq(x, axis, fmt="e4m3"):
    dtype, down = {"e4m3": (ml_dtypes.float8_e4m3fn, 7), "e5m2": (ml_dtypes.float8_e5m2, 14)}[fmt]
    v = np.moveaxis(np.asarray(x, np.float32).astype(ml_dtypes.bfloat16).astype(np.float64), axis, -1)
    blocks = v.reshape(v.shape[:-1] + (-1, 32))
    amax = np.abs(blocks).max(-1, keepdims=True)
    byte = np.maximum(np.where(amax > 0, np.frexp(amax)[1] - 1 + 127, 0) - down, 1)
    scale = np.exp2(byte - 127.0)
    codes = (blocks / scale).astype(np.float32).astype(dtype).astype(np.float64)
    return np.moveaxis((codes * scale).reshape(v.shape), -1, axis)


WIDE = False


def mx_kscale(k):
    if not WIDE:
        return np.ones(k)
    levels = np.array([10, -10, 5, -5, 0])
    if k % 512:
        return np.exp2(np.random.permutation(np.resize(levels, k // 32))).repeat(32)
    a = np.empty((k // 512, 16))
    for p in range(k // 512):
        a[p, :8] = np.random.permutation(np.resize(levels, 8))
        for g in range(8):
            far = levels[np.abs(levels - a[p, g]) >= 10]
            a[p, g + 8] = far[np.random.randint(len(far))]
    return np.exp2(a.ravel()).repeat(32)


def f64(x):
    return np.asarray(x).astype(np.float64)


def striped(idx):
    return np.tile(idx.reshape(-1, 16).T, (8, 1)).astype(np.uint16)


def unstriped(offs):
    return offs[:16].T.reshape(-1).astype(np.int64)


def pack_weight(w):
    k, n = w.shape
    w = f64(np.asarray(w, np.float32).astype(ml_dtypes.bfloat16)).reshape(k // 32, 32, n)
    amax = np.abs(w).max(1)
    byte = np.clip(np.where(amax > 0, np.frexp(amax)[1] - 1 + 127 - 7, 1), 1, 254)
    scaled = (w * np.exp2(127.0 - byte)[:, None, :]).reshape(k, n).astype(np.float32)
    words = np.ascontiguousarray(scaled.reshape(k // 512, 128, 4, n).transpose(0, 1, 3, 2)).astype(ml_dtypes.float8_e4m3fn).view(np.uint8)
    return words, np.ascontiguousarray(byte.astype(np.uint8).reshape(k // 512, 16, n))


def unpack_weight(words, scales):
    g, p, n, _ = words.shape
    vals = np.ascontiguousarray(words).view(ml_dtypes.float8_e4m3fn).astype(np.float64) * np.repeat(np.exp2(scales.astype(np.float64) - 127.0), 8, axis=1)[..., None]
    return vals.transpose(0, 1, 3, 2).reshape(g * 512, n)


E2M1 = np.array([0.0, 0.5, 1.0, 1.5, 2.0, 3.0, 4.0, 6.0, -0.0, -0.5, -1.0, -1.5, -2.0, -3.0, -4.0, -6.0])


def pack_fp4(w):
    k, n = w.shape
    w = f64(np.asarray(w, np.float32).astype(ml_dtypes.bfloat16)).reshape(k // 32, 32, n)
    amax = np.abs(w).max(1)
    mant, ex = np.frexp(amax / 6.0)
    byte = np.clip(np.where(amax > 0, np.where(mant > 0.5, ex, ex - 1) + 127, 1), 1, 254)
    scaled = (w * np.exp2(127.0 - byte)[:, None, :]).reshape(k, n).astype(np.float32)
    c = np.ascontiguousarray(scaled.reshape(k // 512, 128, 4, n).transpose(0, 1, 3, 2)).astype(ml_dtypes.float4_e2m1fn).view(np.uint8) & 0xF
    words = (c[..., 0::2] | (c[..., 1::2] << 4)).reshape(k // 512, 128, 2 * n)
    return np.ascontiguousarray(words), np.ascontiguousarray(byte.astype(np.uint8).reshape(k // 512, 16, n))


def unpack_fp4(words, scales):
    g, _, n = scales.shape
    words = np.ascontiguousarray(words).reshape(g, 128, n, 2)
    nib = np.empty((g, 128, n, 4), np.uint8)
    nib[..., 0::2] = words & 0xF
    nib[..., 1::2] = words >> 4
    vals = E2M1[nib] * np.repeat(np.exp2(scales.astype(np.float64) - 127.0), 8, axis=1)[..., None]
    return vals.transpose(0, 1, 3, 2).reshape(g * 512, n)


def planes(y):
    n, m = y.shape
    v = y.astype(np.float32).astype(ml_dtypes.bfloat16).astype(np.float64).reshape(n // 32, 32, m)
    top = np.abs(v).max(1)
    byte = np.clip(np.where(top > 0, np.frexp(top)[1] - 1 + 127 - 7, 1), 1, 254)
    codes = (v * np.exp2(127.0 - byte)[:, None, :]).reshape(n, m).astype(np.float32).astype(ml_dtypes.float8_e4m3fn).view(np.uint8)
    words = codes.reshape(n // 512, 128, 4, m).transpose(0, 1, 3, 2)
    return np.ascontiguousarray(words), np.ascontiguousarray(byte.astype(np.uint8).reshape(n // 512, 16, m))


K, T, S, N, H, W, C = 512, 2048, 256, 512, 512, 192, 512


def setup_inputs():
    n = np.random.standard_normal
    s = mx_kscale(K)[:, None]
    u = mx_kscale(K)
    packed_xT = pack_weight(n((K, T)) * s)
    packed_w1 = pack_fp4(n((K, H)) / np.sqrt(K) / s)
    packed_w2 = pack_fp4(n((K, H)) / np.sqrt(K) / s)
    packed_w3 = pack_fp4(n((H, N)) / np.sqrt(H) / u[:, None])
    return {
        "x_words": packed_xT[0],
        "x_scales": packed_xT[1],
        "w1_words": packed_w1[0],
        "w1_scales": packed_w1[1],
        "w2_words": packed_w2[0],
        "w2_scales": packed_w2[1],
        "gn": (np.random.uniform(0.5, 1.5, (H, 1)) * u[:, None]).astype(np.float32),
        "w3_words": packed_w3[0],
        "w3_scales": packed_w3[1],
        "gs": (np.random.uniform(0.5, 1.5, (K, 1)) / s).astype(np.float32),
        "offs": striped(np.random.permutation(T)[:S]),
        "two": striped(np.random.permutation(T)[:S]),
        "n1": striped(np.random.permutation(S)[:W]),
        "n2": striped(np.random.permutation(S)[:W]),
        "n3": striped(np.random.permutation(S)),
        "n4": striped(np.random.permutation(S)),
        "cand": striped(np.random.permutation(T)[:C]),
        "n5": striped(np.random.permutation(S)),
        "n6": striped(np.random.permutation(S)),
        "n7": striped(np.random.permutation(S)),
    }


def reference(x_words, x_scales, w1_words, w1_scales, w2_words, w2_scales, gn, w3_words, w3_scales, gs, offs, two, n1, n2, n3, n4, cand, n5, n6, n7):
    x_cand = unpack_weight(x_words, x_scales)[:, unstriped(cand)]
    x_two = unpack_weight(x_words, x_scales)[:, unstriped(two)]
    d = unpack_fp4(w2_words, w2_scales).T @ x_two
    sq = (d) ** 2
    z2 = f64(gs) * (d[:, unstriped(n4)] / (np.sqrt(sq + sq[:, unstriped(n3)] + 0.25)))
    b = 0.0625 * ((x_cand.T @ mxq(z2, 0, "e4m3")))
    xq = unpack_weight(x_words, x_scales)[:, unstriped(offs)]
    y = unpack_fp4(w1_words, w1_scales).T @ xq
    old = y[:, unstriped(n1)]
    pa = y[:, unstriped(n2)]
    ra = old - (0.5 * pa)
    ds = y.copy()
    ds[:, unstriped(n1)] = ra
    z = f64(gn) * ds
    a = unpack_fp4(w3_words, w3_scales).T @ mxq(z, 0, "e4m3")
    out_0 = b * (a[:, unstriped(n5)] - a) + 0.5 * (b[:, unstriped(n7)] * (a[:, unstriped(n6)] - a))
    return (out_0,) + planes(out_0)

@@ -1,0 +1,268 @@
+from contextlib import ExitStack
+
+import concourse.mybir as mybir
+
+K, T, S, W, C = 512, 2048, 256, 192, 512
+FLOPS = 2 * K * 512 * S * 4
+
+F32 = mybir.dt.float32
+BF16 = mybir.dt.bfloat16
+I32 = mybir.dt.int32
+U32 = mybir.dt.uint32
+U16 = mybir.dt.uint16
+U8 = mybir.dt.uint8
+FP8X4 = mybir.dt.float8_e4m3fn_x4
+FP4X4 = mybir.dt.float4_e2m1fn_x4
+COPY = mybir.ActivationFunctionType.Copy
+RSQRT = mybir.ActivationFunctionType.Abs_reciprocal_sqrt
+ADD = mybir.AluOpType.add
+SUB = mybir.AluOpType.subtract
+MULT = mybir.AluOpType.mult
+
+P = 128
+PACK = 4
+SPARE = 8
+HALF = S // 2
+
+
+def load_scale_rows(queues, tile, scales):
+    for q in range(4):
+        queues[q].dma_start(tile[32 * q : 32 * q + 4, :].bitcast(I32), scales[0, 4 * q : 4 * q + 4, :].bitcast(I32))
+
+
+def tile_picked_tfcdflowbkdifrms_none_po_kernel(
+    tc, x_words, x_scales, w1_words, w1_scales, w2_words, w2_scales, gn, w3_words, w3_scales, gs,
+    offs, two, n1, n2, n3, n4, cand, n5, n6, n7, out_0, out_1, out_2,
+):
+    nc = tc.nc
+    with ExitStack() as ctx:
+        sb = ctx.enter_context(tc.tile_pool(name="sb", bufs=1))
+        ps = ctx.enter_context(tc.psum_pool(name="ps", bufs=4))
+
+        def new(name, cols, dtype):
+            return sb.tile([P, cols], dtype, name=name, align_bytes=64)
+
+        def planes(name, cols):
+            return [new("%s%d" % (name, t), cols, F32) for t in range(PACK)]
+
+        def load_list(name, src):
+            tile = sb.tile([P, src.shape[1]], U16, name=name)
+            nc.sync.dma_start(tile[:], src)
+            return tile
+
+        def load_column(queue, name, src):
+            tile = new(name, PACK, F32)
+            queue.dma_start(tile[:], src.rearrange("(p t) o -> p (t o)", t=PACK))
+            return tile
+
+        def load_fp4_words(queue, name, src):
+            tile = new(name, 2 * K, U8)
+            queue.dma_start(tile[:].bitcast(I32), src[0].bitcast(I32))
+            return tile
+
+        def zeroed_plane(engine, name, cols):
+            tile = new(name, cols, U8)
+            engine.memset(tile[:].bitcast(I32), 0)
+            return tile
+
+        def deal_fp4_words(name, src):
+            tile = new(name, 2 * K, U8)
+            nc.vector.tensor_copy(
+                tile[:].rearrange("p (t m e) -> p t m e", t=PACK, e=2),
+                src[:].rearrange("p (m t e) -> p t m e", t=PACK, e=2),
+            )
+            return tile
+
+        def deal(name, src, dtype, view):
+            tile = new(name, K, dtype)
+            nc.vector.tensor_copy(
+                tile[:].bitcast(view).rearrange("p (t m) -> p t m", t=PACK),
+                src[:].bitcast(view).rearrange("p (m t) -> p t m", t=PACK),
+            )
+            return tile
+
+        def gather(name, tag, table, lst, dtype):
+            tile = sb.tile([P, 16 * lst.shape[1]], dtype, name=name, tag=tag, align_bytes=64)
+            nc.vector.tensor_copy(tile[:], table.indirect(lst[:]))
+            return tile
+
+        def product(tag, per_bank, words, width, view, scales, rhs, rhs_scales):
+            banks = []
+            for t in range(PACK):
+                if t % per_bank == 0:
+                    banks.append(ps.tile([P, per_bank * S], F32, name="%s%d" % (tag, t), tag=tag))
+                nc.tensor.matmul_mx(
+                    out=banks[-1][:, S * (t % per_bank) : S * (t % per_bank + 1)],
+                    lhsT=words[:, width * t : width * (t + 1)].bitcast(view),
+                    lhsT_scale=scales[:, P * t : P * (t + 1)],
+                    rhs=rhs.bitcast(FP8X4),
+                    rhs_scale=rhs_scales,
+                    start=True,
+                    stop=True,
+                )
+            return banks
+
+        def quantize(words, scales, grouped):
+            nc.vector.quantize_mx(out=words.bitcast(FP8X4), scales=scales, in_=grouped)
+
+        w1s = zeroed_plane(nc.gpsimd, "w1s", K)
+        xs = zeroed_plane(nc.vector, "xs", T)
+        l_offs = load_list("l_offs", offs)
+        w1w = load_fp4_words(nc.scalar, "w1w", w1_words)
+        load_scale_rows([nc.sync, nc.scalar] * 2, w1s, w1_scales)
+        xw = new("xw", T, I32)
+        nc.sync.dma_start(xw[:], x_words[0].rearrange("p c r -> p (c r)").bitcast(I32))
+        load_scale_rows([nc.scalar] * 4, xs, x_scales)
+        gn_t = load_column(nc.sync, "gn_t", gn)
+        l_n1 = load_list("l_n1", n1)
+        l_n2 = load_list("l_n2", n2)
+        w2s = zeroed_plane(nc.gpsimd, "w2s", K)
+        w3s = zeroed_plane(nc.gpsimd, "w3s", K)
+        l_two = load_list("l_two", two)
+        w2w = load_fp4_words(nc.sync, "w2w", w2_words)
+        load_scale_rows([nc.sync] * 4, w2s, w2_scales)
+        w3w = load_fp4_words(nc.sync, "w3w", w3_words)
+        load_scale_rows([nc.sync] * 4, w3s, w3_scales)
+        l_cand = load_list("l_cand", cand)
+        l_n3 = load_list("l_n3", n3)
+        l_n4 = load_list("l_n4", n4)
+        gs_t = load_column(nc.sync, "gs_t", gs)
+        l_n5 = load_list("l_n5", n5)
+        l_n6 = load_list("l_n6", n6)
+        l_n7 = load_list("l_n7", n7)
+
+        xw_u = xw[:].bitcast(U32)
+        ROW = PACK * S
+        dsq = new("dsq", 2 * ROW + S, F32)
+        a = new("a", ROW + S, F32)
+        nc.gpsimd.memset(dsq[:, 2 * ROW :], 0.0)
+        nc.gpsimd.memset(a[:, ROW:], 0.0)
+        z_s = zeroed_plane(nc.gpsimd, "z_s", S)
+        z2_s = zeroed_plane(nc.gpsimd, "z2_s", S)
+        o_s = zeroed_plane(nc.gpsimd, "o_s", S)
+        one = lambda t: slice(S * t, S * (t + 1))
+        pair = lambda i: slice(2 * S * i, 2 * S * (i + 1))
+        window = lambda tile, t: tile[:, S * t : S * (t + 2)]
+
+        w1d = deal_fp4_words("w1d", w1w)
+        w1sd = deal("w1sd", w1s, U8, U8)
+        xq_s = gather("xq_s", "picked_scales", xs[:], l_offs, U8)
+        xq_w = gather("xq_w", "picked_words", xw_u, l_offs, U32)
+        y_ps = product("ya", 1, w1d, 2 * P, FP4X4, w1sd, xq_w[:], xq_s[:])
+        z = planes("z", S)
+        for t in range(PACK):
+            nc.vector.tensor_scalar(z[t][:], y_ps[t][:], gn_t[:, t : t + 1], None, MULT)
+        old = new("old", PACK * W, F32)
+        pa = new("pa", PACK * W, F32)
+        ra = new("ra", PACK * W, F32)
+        for t in range(PACK):
+            cols = slice(W * t, W * (t + 1))
+            nc.scalar.activation(old[:, cols], z[t][:].indirect(l_n1[:]), COPY)
+            nc.scalar.activation(pa[:, cols], z[t][:].indirect(l_n2[:]), COPY)
+
+        x2_w = gather("x2_w", "picked_words", xw_u, l_two, U32)
+        x2_s = gather("x2_s", "picked_scales", xs[:], l_two, U8)
+        nc.vector.scalar_tensor_tensor(ra[:, : 2 * W], pa[:, : 2 * W], -0.5, old[:, : 2 * W], MULT, ADD)
+        w2d = deal_fp4_words("w2d", w2w)
+        w2sd = deal("w2sd", w2s, U8, U8)
+        d_ps = product("db", 2, w2d, 2 * P, FP4X4, w2sd, x2_w[:], x2_s[:])
+        nc.vector.scalar_tensor_tensor(ra[:, 2 * W :], pa[:, 2 * W :], -0.5, old[:, 2 * W :], MULT, ADD)
+        for t in range(PACK):
+            nc.scalar.activation(z[t][:].indirect(l_n1[:]), ra[:, W * t : W * (t + 1)], COPY)
+        for i in range(2):
+            nc.vector.tensor_copy(dsq[:, pair(i)], d_ps[i][:])
+        for i in range(2):
+            nc.vector.tensor_tensor(dsq[:, pair(2 + i)], d_ps[i][:], dsq[:, pair(i)], MULT)
+        w3d = deal_fp4_words("w3d", w3w)
+        w3sd = deal("w3sd", w3s, U8, U8)
+
+        z_r = new("z_r", ROW, BF16)
+        for t in range(PACK - 1):
+            nc.vector.tensor_copy(z_r[:, one(t)], z[t][:])
+        xc_w = gather("xc_w", "picked_words", xw_u, l_cand, U32)
+        nc.vector.tensor_copy(z_r[:, one(PACK - 1)], z[PACK - 1][:])
+        xc_wd = deal("xc_wd", xc_w, U32, I32)
+        z_bf = new("z_bf", ROW, BF16)
+        nc.vector.tensor_copy(
+            z_bf[:].rearrange("p (c t) -> p c t", t=PACK), z_r[:].rearrange("p (t c) -> p c t", t=PACK)
+        )
+        sq_n3 = new("sq_n3", ROW, F32)
+        den = new("den", ROW, F32)
+        for t in range(PACK):
+            nc.scalar.activation(sq_n3[:, one(t)], window(dsq, PACK + t).indirect(l_n3[:]), COPY)
+        nc.vector.scalar_tensor_tensor(den[:, pair(0)], sq_n3[:, pair(0)], 0.25, dsq[:, pair(2)], ADD, ADD)
+        z_w = new("z_w", S, U32)
+        quantize(z_w[:], z_s[:], z_bf[:])
+        a_ps = product("ya", 2, w3d, 2 * P, FP4X4, w3sd, z_w[:], z_s[:])
+        nc.vector.scalar_tensor_tensor(den[:, pair(1)], sq_n3[:, pair(1)], 0.25, dsq[:, pair(3)], ADD, ADD)
+        xc_s = gather("xc_s", "picked_scales", xs[:], l_cand, U8)
+        for i in range(2):
+            nc.vector.tensor_copy(a[:, pair(i)], a_ps[i][:])
+        xc_sd = deal("xc_sd", xc_s, U8, U8)
+
+        inv = new("inv", ROW, F32)
+        d4_01 = new("d4_01", 2 * S, F32)
+        d4 = [d4_01[:, one(0)], d4_01[:, one(1)], den[:, one(0)], den[:, one(2)]]
+        z2 = new("z2", ROW, F32)
+        for t in range(PACK):
+            nc.scalar.activation(d4[t], window(dsq, t).indirect(l_n4[:]), COPY)
+            if t < 2:
+                nc.scalar.activation(inv[:, pair(t)], den[:, pair(t)], RSQRT)
+        for t in range(PACK):
+            nc.vector.scalar_tensor_tensor(z2[:, one(t)], d4[t], gs_t[:, t : t + 1], inv[:, one(t)], MULT, MULT)
+        z2_bf = new("z2_bf", ROW, BF16)
+        nc.vector.tensor_copy(
+            z2_bf[:].rearrange("p (c t) -> p c t", t=PACK), z2[:].rearrange("p (t c) -> p c t", t=PACK)
+        )
+        z2_w = new("z2_w", S, U32)
+        quantize(z2_w[:], z2_s[:], z2_bf[:])
+        b_ps = product("db", 2, xc_wd, P, FP8X4, xc_sd, z2_w[:], z2_s[:])
+
+        a5 = dsq[:, 3 * S : 3 * S + ROW]
+        a6 = new("a6", ROW, F32)
+        u = new("u", ROW, F32)
+        b = new("b", ROW, F32)
+        for t in range(PACK):
+            nc.scalar.activation(a5[:, one(t)], window(a, t).indirect(l_n5[:]), COPY)
+        for t in range(PACK):
+            nc.scalar.activation(a6[:, one(t)], window(a, t).indirect(l_n6[:]), COPY)
+        for i in range(2):
+            nc.vector.tensor_tensor(a5[:, pair(i)], a5[:, pair(i)], a_ps[i][:], SUB)
+            nc.vector.tensor_scalar(b[:, pair(i)], b_ps[i][:], 0.0625, None, MULT)
+        for i in range(2):
+            nc.vector.scalar_tensor_tensor(u[:, pair(i)], b_ps[i][:], 0.0625, a5[:, pair(i)], MULT, MULT)
+            nc.vector.tensor_tensor(a6[:, pair(i)], a6[:, pair(i)], a_ps[i][:], SUB)
+
+        b7 = new("b7", ROW, F32)
+        res = new("res", ROW, F32)
+        res_bf = new("res_bf", ROW, BF16)
+        o_w = new("o_w", S, U32)
+        by_t = lambda tile: tile[:].rearrange("p (t c) -> p t c", t=PACK)
+        out_rows = out_0.rearrange("(p t) c -> p t c", t=PACK)
+        for h in range(2):
+            cols = slice(HALF * h, HALF * (h + 1))
+            for t in range(PACK):
+                nc.scalar.activation(
+                    by_t(b7)[:, t, cols], b[:, one(t)].indirect(l_n7[:, HALF // 16 * h : HALF // 16 * (h + 1)]), COPY
+                )
+            step = PACK if h == 0 else 2
+            for t in range(0, PACK, step):
+                nc.vector.scalar_tensor_tensor(
+                    by_t(b7)[:, t : t + step, cols], by_t(b7)[:, t : t + step, cols], 0.5, by_t(a6)[:, t : t + step, cols], MULT, MULT
+                )
+            for t in range(0, PACK, step):
+                nc.vector.tensor_tensor(
+                    by_t(res)[:, t : t + step, cols], by_t(b7)[:, t : t + step, cols], by_t(u)[:, t : t + step, cols], ADD
+                )
+            nc.sync.dma_start(out_rows[:, :, cols], by_t(res)[:, :, cols])
+            grouped = res_bf[:, PACK * HALF * h : PACK * HALF * (h + 1)]
+            nc.vector.tensor_copy(
+                grouped.rearrange("p (c t) -> p c t", t=PACK), by_t(res)[:, :, cols].rearrange("p t c -> p c t")
+            )
+            quantize(o_w[:, cols], o_s[:, cols], grouped)
+            (nc.sync if h == 0 else nc.scalar).dma_start(
+                out_1[0].rearrange("p c r -> p (c r)").bitcast(I32)[:, cols], o_w[:, cols].bitcast(I32)
+            )
+        for q in range(4):
+            queue = nc.sync if q % 2 == 0 else nc.scalar
+            queue.dma_start(out_2[0, 4 * q : 4 * q + 4, :].bitcast(I32), o_s[32 * q : 32 * q + 4, :].bitcast(I32))

@@ -112,6 +112,10 @@ def tile_picked_tfcdflowbkdifrms_none_po_kernel(
         load_scale_rows([nc.sync, nc.scalar] * 2, w1s, w1_scales)
         xw = new("xw", T, I32)
         nc.sync.dma_start(xw[:], x_words[0].rearrange("p c r -> p (c r)").bitcast(I32))
+        warm_in = new("warm_in", 1, F32)
+        warm_out = new("warm_out", 1, F32)
+        nc.vector.memset(warm_in[:], 1.0)
+        nc.scalar.activation(warm_out[:], warm_in[:], RSQRT)
         load_scale_rows([nc.scalar] * 4, xs, x_scales)
         gn_t = load_column(nc.sync, "gn_t", gn)
         l_n1 = load_list("l_n1", n1)

@@ -65,8 +65,8 @@ def tile_picked_tfcdflowbkdifrms_none_po_kernel(
             engine.memset(tile[:].bitcast(I32), 0)
             return tile
 
-        def deal_fp4_words(name, src):
-            tile = new(name, 2 * K, U8)
+        def deal_fp4_words(name, src, tag):
+            tile = sb.tile([P, 2 * K], U8, name=name, tag=tag, align_bytes=64)
             nc.vector.tensor_copy(
                 tile[:].rearrange("p (t m e) -> p t m e", t=PACK, e=2),
                 src[:].rearrange("p (m t e) -> p t m e", t=PACK, e=2),
@@ -74,7 +74,7 @@ def tile_picked_tfcdflowbkdifrms_none_po_kernel(
             return tile
 
         def deal(name, src, dtype, view):
-            tile = new(name, K, dtype)
+            tile = sb.tile([P, K], dtype, name=name, tag=name, align_bytes=64)
             nc.vector.tensor_copy(
                 tile[:].bitcast(view).rearrange("p (t m) -> p t m", t=PACK),
                 src[:].bitcast(view).rearrange("p (m t) -> p t m", t=PACK),
@@ -107,6 +107,8 @@ def tile_picked_tfcdflowbkdifrms_none_po_kernel(
 
         w1s = zeroed_plane(nc.gpsimd, "w1s", K)
         xs = zeroed_plane(nc.vector, "xs", T)
+        w2s = zeroed_plane(nc.gpsimd, "w2s", K)
+        w3s = zeroed_plane(nc.gpsimd, "w3s", K)
         l_offs = load_list("l_offs", offs)
         w1w = load_fp4_words(nc.scalar, "w1w", w1_words)
         load_scale_rows([nc.sync, nc.scalar] * 2, w1s, w1_scales)
@@ -117,24 +119,21 @@ def tile_picked_tfcdflowbkdifrms_none_po_kernel(
         nc.vector.memset(warm_in[:], 1.0)
         nc.scalar.activation(warm_out[:], warm_in[:], RSQRT)
         load_scale_rows([nc.scalar] * 4, xs, x_scales)
-        gn_t = load_column(nc.sync, "gn_t", gn)
         l_n1 = load_list("l_n1", n1)
         l_n2 = load_list("l_n2", n2)
-        w2s = zeroed_plane(nc.gpsimd, "w2s", K)
-        w3s = zeroed_plane(nc.gpsimd, "w3s", K)
         l_two = load_list("l_two", two)
         w2w = load_fp4_words(nc.sync, "w2w", w2_words)
         load_scale_rows([nc.sync] * 4, w2s, w2_scales)
-        w3w = load_fp4_words(nc.sync, "w3w", w3_words)
-        load_scale_rows([nc.sync] * 4, w3s, w3_scales)
+        gn_t = load_column(nc.sync, "gn_t", gn)
         l_cand = load_list("l_cand", cand)
         l_n3 = load_list("l_n3", n3)
+        w3w = load_fp4_words(nc.sync, "w3w", w3_words)
         l_n4 = load_list("l_n4", n4)
+        load_scale_rows([nc.sync] * 4, w3s, w3_scales)
         gs_t = load_column(nc.sync, "gs_t", gs)
         l_n5 = load_list("l_n5", n5)
         l_n6 = load_list("l_n6", n6)
         l_n7 = load_list("l_n7", n7)
-
         xw_u = xw[:].bitcast(U32)
         ROW = PACK * S
         dsq = new("dsq", 2 * ROW + S, F32)
@@ -148,14 +147,15 @@ def tile_picked_tfcdflowbkdifrms_none_po_kernel(
         pair = lambda i: slice(2 * S * i, 2 * S * (i + 1))
         window = lambda tile, t: tile[:, S * t : S * (t + 2)]
 
-        w1d = deal_fp4_words("w1d", w1w)
+        w1d = deal_fp4_words("w1d", w1w, "w1d")
         w1sd = deal("w1sd", w1s, U8, U8)
         xq_s = gather("xq_s", "picked_scales", xs[:], l_offs, U8)
         xq_w = gather("xq_w", "picked_words", xw_u, l_offs, U32)
         y_ps = product("ya", 1, w1d, 2 * P, FP4X4, w1sd, xq_w[:], xq_s[:])
         z = planes("z", S)
-        for t in range(PACK):
-            nc.vector.tensor_scalar(z[t][:], y_ps[t][:], gn_t[:, t : t + 1], None, MULT)
+        nc.scalar.copy(z[0][:], y_ps[0][:])
+        for t in range(1, PACK):
+            nc.vector.tensor_copy(z[t][:], y_ps[t][:])
         old = new("old", PACK * W, F32)
         pa = new("pa", PACK * W, F32)
         ra = new("ra", PACK * W, F32)
@@ -167,7 +167,7 @@ def tile_picked_tfcdflowbkdifrms_none_po_kernel(
         x2_w = gather("x2_w", "picked_words", xw_u, l_two, U32)
         x2_s = gather("x2_s", "picked_scales", xs[:], l_two, U8)
         nc.vector.scalar_tensor_tensor(ra[:, : 2 * W], pa[:, : 2 * W], -0.5, old[:, : 2 * W], MULT, ADD)
-        w2d = deal_fp4_words("w2d", w2w)
+        w2d = deal_fp4_words("w2d", w2w, "w2d")
         w2sd = deal("w2sd", w2s, U8, U8)
         d_ps = product("db", 2, w2d, 2 * P, FP4X4, w2sd, x2_w[:], x2_s[:])
         nc.vector.scalar_tensor_tensor(ra[:, 2 * W :], pa[:, 2 * W :], -0.5, old[:, 2 * W :], MULT, ADD)
@@ -177,32 +177,30 @@ def tile_picked_tfcdflowbkdifrms_none_po_kernel(
             nc.vector.tensor_copy(dsq[:, pair(i)], d_ps[i][:])
         for i in range(2):
             nc.vector.tensor_tensor(dsq[:, pair(2 + i)], d_ps[i][:], dsq[:, pair(i)], MULT)
-        w3d = deal_fp4_words("w3d", w3w)
+        w3d = deal_fp4_words("w3d", w3w, "w3d")
         w3sd = deal("w3sd", w3s, U8, U8)
 
         z_r = new("z_r", ROW, BF16)
-        for t in range(PACK - 1):
-            nc.vector.tensor_copy(z_r[:, one(t)], z[t][:])
+        for t in range(PACK):
+            nc.gpsimd.tensor_scalar(z_r[:, one(t)], z[t][:], gn_t[:, t : t + 1], 0.0, MULT, ADD)
         xc_w = gather("xc_w", "picked_words", xw_u, l_cand, U32)
-        nc.vector.tensor_copy(z_r[:, one(PACK - 1)], z[PACK - 1][:])
+        xc_s = gather("xc_s", "picked_scales", xs[:], l_cand, U8)
         xc_wd = deal("xc_wd", xc_w, U32, I32)
-        z_bf = new("z_bf", ROW, BF16)
+        z_bf = sb.tile([P, ROW], BF16, name="z_bf", tag="w2d", align_bytes=64)
         nc.vector.tensor_copy(
             z_bf[:].rearrange("p (c t) -> p c t", t=PACK), z_r[:].rearrange("p (t c) -> p c t", t=PACK)
         )
+        xc_sd = deal("xc_sd", xc_s, U8, U8)
+        z_w = new("z_w", S, U32)
+        quantize(z_w[:], z_s[:], z_bf[:])
+        a_ps = product("ya", 2, w3d, 2 * P, FP4X4, w3sd, z_w[:], z_s[:])
         sq_n3 = new("sq_n3", ROW, F32)
         den = new("den", ROW, F32)
         for t in range(PACK):
             nc.scalar.activation(sq_n3[:, one(t)], window(dsq, PACK + t).indirect(l_n3[:]), COPY)
-        nc.vector.scalar_tensor_tensor(den[:, pair(0)], sq_n3[:, pair(0)], 0.25, dsq[:, pair(2)], ADD, ADD)
-        z_w = new("z_w", S, U32)
-        quantize(z_w[:], z_s[:], z_bf[:])
-        a_ps = product("ya", 2, w3d, 2 * P, FP4X4, w3sd, z_w[:], z_s[:])
-        nc.vector.scalar_tensor_tensor(den[:, pair(1)], sq_n3[:, pair(1)], 0.25, dsq[:, pair(3)], ADD, ADD)
-        xc_s = gather("xc_s", "picked_scales", xs[:], l_cand, U8)
         for i in range(2):
+            nc.vector.scalar_tensor_tensor(den[:, pair(i)], sq_n3[:, pair(i)], 0.25, dsq[:, pair(2 + i)], ADD, ADD)
             nc.vector.tensor_copy(a[:, pair(i)], a_ps[i][:])
-        xc_sd = deal("xc_sd", xc_s, U8, U8)
 
         inv = new("inv", ROW, F32)
         d4_01 = new("d4_01", 2 * S, F32)
@@ -214,7 +212,7 @@ def tile_picked_tfcdflowbkdifrms_none_po_kernel(
                 nc.scalar.activation(inv[:, pair(t)], den[:, pair(t)], RSQRT)
         for t in range(PACK):
             nc.vector.scalar_tensor_tensor(z2[:, one(t)], d4[t], gs_t[:, t : t + 1], inv[:, one(t)], MULT, MULT)
-        z2_bf = new("z2_bf", ROW, BF16)
+        z2_bf = sb.tile([P, ROW], BF16, name="z2_bf", tag="z2_bf", align_bytes=64)
         nc.vector.tensor_copy(
             z2_bf[:].rearrange("p (c t) -> p c t", t=PACK), z2[:].rearrange("p (t c) -> p c t", t=PACK)
         )
@@ -225,17 +223,23 @@ def tile_picked_tfcdflowbkdifrms_none_po_kernel(
         a5 = dsq[:, 3 * S : 3 * S + ROW]
         a6 = new("a6", ROW, F32)
         u = new("u", ROW, F32)
+        v = new("v", ROW, F32)
         b = new("b", ROW, F32)
         for t in range(PACK):
             nc.scalar.activation(a5[:, one(t)], window(a, t).indirect(l_n5[:]), COPY)
         for t in range(PACK):
             nc.scalar.activation(a6[:, one(t)], window(a, t).indirect(l_n6[:]), COPY)
+        e5 = [
+            sb.tile([P, 2 * S], F32, name="e5_0", tag="z2_bf", align_bytes=64),
+            sb.tile([P, 2 * S], F32, name="e5_1", tag="xc_wd", align_bytes=64),
+        ]
+        nc.vector.tensor_tensor(e5[0][:], a5[:, pair(0)], a_ps[0][:], SUB)
         for i in range(2):
-            nc.vector.tensor_tensor(a5[:, pair(i)], a5[:, pair(i)], a_ps[i][:], SUB)
-            nc.vector.tensor_scalar(b[:, pair(i)], b_ps[i][:], 0.0625, None, MULT)
+            nc.vector.tensor_scalar(b[:, pair(i)], b_ps[i][:], 0.5 * 0.0625, None, MULT)
+        nc.vector.tensor_tensor(e5[1][:], a5[:, pair(1)], a_ps[1][:], SUB)
         for i in range(2):
-            nc.vector.scalar_tensor_tensor(u[:, pair(i)], b_ps[i][:], 0.0625, a5[:, pair(i)], MULT, MULT)
-            nc.vector.tensor_tensor(a6[:, pair(i)], a6[:, pair(i)], a_ps[i][:], SUB)
+            nc.vector.scalar_tensor_tensor(u[:, pair(i)], b_ps[i][:], 0.0625, e5[i][:], MULT, MULT)
+            nc.gpsimd.tensor_tensor(v[:, pair(i)], a6[:, pair(i)], a[:, pair(i)], SUB)
 
         b7 = new("b7", ROW, F32)
         res = new("res", ROW, F32)
@@ -249,10 +253,10 @@ def tile_picked_tfcdflowbkdifrms_none_po_kernel(
                 nc.scalar.activation(
                     by_t(b7)[:, t, cols], b[:, one(t)].indirect(l_n7[:, HALF // 16 * h : HALF // 16 * (h + 1)]), COPY
                 )
-            step = PACK if h == 0 else 2
+            step = 2
             for t in range(0, PACK, step):
-                nc.vector.scalar_tensor_tensor(
-                    by_t(b7)[:, t : t + step, cols], by_t(b7)[:, t : t + step, cols], 0.5, by_t(a6)[:, t : t + step, cols], MULT, MULT
+                nc.vector.tensor_tensor(
+                    by_t(b7)[:, t : t + step, cols], by_t(b7)[:, t : t + step, cols], by_t(v)[:, t : t + step, cols], MULT
                 )
             for t in range(0, PACK, step):
                 nc.vector.tensor_tensor(

from contextlib import ExitStack

import concourse.mybir as mybir

K, T, S, W, C = 512, 2048, 256, 192, 512
FLOPS = 2 * K * 512 * S * 4

F32 = mybir.dt.float32
BF16 = mybir.dt.bfloat16
I32 = mybir.dt.int32
U32 = mybir.dt.uint32
U16 = mybir.dt.uint16
U8 = mybir.dt.uint8
FP8X4 = mybir.dt.float8_e4m3fn_x4
FP4X4 = mybir.dt.float4_e2m1fn_x4
COPY = mybir.ActivationFunctionType.Copy
RSQRT = mybir.ActivationFunctionType.Abs_reciprocal_sqrt
ADD = mybir.AluOpType.add
SUB = mybir.AluOpType.subtract
MULT = mybir.AluOpType.mult

P = 128
PACK = 4
SPARE = 8
HALF = S // 2


def load_scale_rows(queues, tile, scales):
    for q in range(4):
        queues[q].dma_start(tile[32 * q : 32 * q + 4, :].bitcast(I32), scales[0, 4 * q : 4 * q + 4, :].bitcast(I32))


def tile_picked_tfcdflowbkdifrms_none_po_kernel(
    tc, x_words, x_scales, w1_words, w1_scales, w2_words, w2_scales, gn, w3_words, w3_scales, gs,
    offs, two, n1, n2, n3, n4, cand, n5, n6, n7, out_0, out_1, out_2,
):
    nc = tc.nc
    with ExitStack() as ctx:
        sb = ctx.enter_context(tc.tile_pool(name="sb", bufs=1))
        ps = ctx.enter_context(tc.psum_pool(name="ps", bufs=4))

        def new(name, cols, dtype):
            return sb.tile([P, cols], dtype, name=name, align_bytes=64)

        def planes(name, cols):
            return [new("%s%d" % (name, t), cols, F32) for t in range(PACK)]

        def load_list(name, src):
            tile = sb.tile([P, src.shape[1]], U16, name=name)
            nc.sync.dma_start(tile[:], src)
            return tile

        def load_column(queue, name, src):
            tile = new(name, PACK, F32)
            queue.dma_start(tile[:], src.rearrange("(p t) o -> p (t o)", t=PACK))
            return tile

        def load_fp4_words(queue, name, src):
            tile = new(name, 2 * K, U8)
            queue.dma_start(tile[:].bitcast(I32), src[0].bitcast(I32))
            return tile

        def zeroed_plane(engine, name, cols):
            tile = new(name, cols, U8)
            engine.memset(tile[:].bitcast(I32), 0)
            return tile

        def deal_fp4_words(name, src, tag):
            tile = sb.tile([P, 2 * K], U8, name=name, tag=tag, align_bytes=64)
            nc.vector.tensor_copy(
                tile[:].rearrange("p (t m e) -> p t m e", t=PACK, e=2),
                src[:].rearrange("p (m t e) -> p t m e", t=PACK, e=2),
            )
            return tile

        def deal(name, src, dtype, view):
            tile = sb.tile([P, K], dtype, name=name, tag=name, align_bytes=64)
            nc.vector.tensor_copy(
                tile[:].bitcast(view).rearrange("p (t m) -> p t m", t=PACK),
                src[:].bitcast(view).rearrange("p (m t) -> p t m", t=PACK),
            )
            return tile

        def gather(name, tag, table, lst, dtype):
            tile = sb.tile([P, 16 * lst.shape[1]], dtype, name=name, tag=tag, align_bytes=64)
            nc.vector.tensor_copy(tile[:], table.indirect(lst[:]))
            return tile

        def product(tag, per_bank, words, width, view, scales, rhs, rhs_scales):
            banks = []
            for t in range(PACK):
                if t % per_bank == 0:
                    banks.append(ps.tile([P, per_bank * S], F32, name="%s%d" % (tag, t), tag=tag))
                nc.tensor.matmul_mx(
                    out=banks[-1][:, S * (t % per_bank) : S * (t % per_bank + 1)],
                    lhsT=words[:, width * t : width * (t + 1)].bitcast(view),
                    lhsT_scale=scales[:, P * t : P * (t + 1)],
                    rhs=rhs.bitcast(FP8X4),
                    rhs_scale=rhs_scales,
                    start=True,
                    stop=True,
                )
            return banks

        def quantize(words, scales, grouped):
            nc.vector.quantize_mx(out=words.bitcast(FP8X4), scales=scales, in_=grouped)

        w1s = zeroed_plane(nc.gpsimd, "w1s", K)
        xs = zeroed_plane(nc.vector, "xs", T)
        w2s = zeroed_plane(nc.gpsimd, "w2s", K)
        w3s = zeroed_plane(nc.gpsimd, "w3s", K)
        l_offs = load_list("l_offs", offs)
        w1w = load_fp4_words(nc.scalar, "w1w", w1_words)
        load_scale_rows([nc.sync, nc.scalar] * 2, w1s, w1_scales)
        xw = new("xw", T, I32)
        nc.sync.dma_start(xw[:], x_words[0].rearrange("p c r -> p (c r)").bitcast(I32))
        warm_in = new("warm_in", 1, F32)
        warm_out = new("warm_out", 1, F32)
        nc.vector.memset(warm_in[:], 1.0)
        nc.scalar.activation(warm_out[:], warm_in[:], RSQRT)
        load_scale_rows([nc.scalar] * 4, xs, x_scales)
        l_n1 = load_list("l_n1", n1)
        l_n2 = load_list("l_n2", n2)
        l_two = load_list("l_two", two)
        w2w = load_fp4_words(nc.sync, "w2w", w2_words)
        load_scale_rows([nc.sync] * 4, w2s, w2_scales)
        gn_t = load_column(nc.sync, "gn_t", gn)
        l_cand = load_list("l_cand", cand)
        l_n3 = load_list("l_n3", n3)
        w3w = load_fp4_words(nc.sync, "w3w", w3_words)
        l_n4 = load_list("l_n4", n4)
        load_scale_rows([nc.sync] * 4, w3s, w3_scales)
        gs_t = load_column(nc.sync, "gs_t", gs)
        l_n5 = load_list("l_n5", n5)
        l_n6 = load_list("l_n6", n6)
        l_n7 = load_list("l_n7", n7)
        xw_u = xw[:].bitcast(U32)
        ROW = PACK * S
        dsq = new("dsq", 2 * ROW + S, F32)
        a = new("a", ROW + S, F32)
        nc.gpsimd.memset(dsq[:, 2 * ROW :], 0.0)
        nc.gpsimd.memset(a[:, ROW:], 0.0)
        z_s = zeroed_plane(nc.gpsimd, "z_s", S)
        z2_s = zeroed_plane(nc.gpsimd, "z2_s", S)
        o_s = zeroed_plane(nc.gpsimd, "o_s", S)
        one = lambda t: slice(S * t, S * (t + 1))
        pair = lambda i: slice(2 * S * i, 2 * S * (i + 1))
        window = lambda tile, t: tile[:, S * t : S * (t + 2)]

        w1d = deal_fp4_words("w1d", w1w, "w1d")
        w1sd = deal("w1sd", w1s, U8, U8)
        xq_s = gather("xq_s", "picked_scales", xs[:], l_offs, U8)
        xq_w = gather("xq_w", "picked_words", xw_u, l_offs, U32)
        y_ps = product("ya", 1, w1d, 2 * P, FP4X4, w1sd, xq_w[:], xq_s[:])
        z = planes("z", S)
        nc.scalar.copy(z[0][:], y_ps[0][:])
        for t in range(1, PACK):
            nc.vector.tensor_copy(z[t][:], y_ps[t][:])
        old = new("old", PACK * W, F32)
        pa = new("pa", PACK * W, F32)
        ra = new("ra", PACK * W, F32)
        for t in range(PACK):
            cols = slice(W * t, W * (t + 1))
            nc.scalar.activation(old[:, cols], z[t][:].indirect(l_n1[:]), COPY)
            nc.scalar.activation(pa[:, cols], z[t][:].indirect(l_n2[:]), COPY)

        x2_w = gather("x2_w", "picked_words", xw_u, l_two, U32)
        x2_s = gather("x2_s", "picked_scales", xs[:], l_two, U8)
        nc.vector.scalar_tensor_tensor(ra[:, : 2 * W], pa[:, : 2 * W], -0.5, old[:, : 2 * W], MULT, ADD)
        w2d = deal_fp4_words("w2d", w2w, "w2d")
        w2sd = deal("w2sd", w2s, U8, U8)
        d_ps = product("db", 2, w2d, 2 * P, FP4X4, w2sd, x2_w[:], x2_s[:])
        nc.vector.scalar_tensor_tensor(ra[:, 2 * W :], pa[:, 2 * W :], -0.5, old[:, 2 * W :], MULT, ADD)
        for t in range(PACK):
            nc.scalar.activation(z[t][:].indirect(l_n1[:]), ra[:, W * t : W * (t + 1)], COPY)
        for i in range(2):
            nc.vector.tensor_copy(dsq[:, pair(i)], d_ps[i][:])
        for i in range(2):
            nc.vector.tensor_tensor(dsq[:, pair(2 + i)], d_ps[i][:], dsq[:, pair(i)], MULT)
        w3d = deal_fp4_words("w3d", w3w, "w3d")
        w3sd = deal("w3sd", w3s, U8, U8)

        z_r = new("z_r", ROW, BF16)
        for t in range(PACK):
            nc.gpsimd.tensor_scalar(z_r[:, one(t)], z[t][:], gn_t[:, t : t + 1], 0.0, MULT, ADD)
        xc_w = gather("xc_w", "picked_words", xw_u, l_cand, U32)
        xc_s = gather("xc_s", "picked_scales", xs[:], l_cand, U8)
        xc_wd = deal("xc_wd", xc_w, U32, I32)
        z_bf = sb.tile([P, ROW], BF16, name="z_bf", tag="w2d", align_bytes=64)
        nc.vector.tensor_copy(
            z_bf[:].rearrange("p (c t) -> p c t", t=PACK), z_r[:].rearrange("p (t c) -> p c t", t=PACK)
        )
        xc_sd = deal("xc_sd", xc_s, U8, U8)
        z_w = new("z_w", S, U32)
        quantize(z_w[:], z_s[:], z_bf[:])
        a_ps = product("ya", 2, w3d, 2 * P, FP4X4, w3sd, z_w[:], z_s[:])
        sq_n3 = new("sq_n3", ROW, F32)
        den = new("den", ROW, F32)
        for t in range(PACK):
            nc.scalar.activation(sq_n3[:, one(t)], window(dsq, PACK + t).indirect(l_n3[:]), COPY)
        for i in range(2):
            nc.vector.scalar_tensor_tensor(den[:, pair(i)], sq_n3[:, pair(i)], 0.25, dsq[:, pair(2 + i)], ADD, ADD)
            nc.vector.tensor_copy(a[:, pair(i)], a_ps[i][:])

        inv = new("inv", ROW, F32)
        d4_01 = new("d4_01", 2 * S, F32)
        d4 = [d4_01[:, one(0)], d4_01[:, one(1)], den[:, one(0)], den[:, one(2)]]
        z2 = new("z2", ROW, F32)
        for t in range(PACK):
            nc.scalar.activation(d4[t], window(dsq, t).indirect(l_n4[:]), COPY)
            if t < 2:
                nc.scalar.activation(inv[:, pair(t)], den[:, pair(t)], RSQRT)
        for t in range(PACK):
            nc.vector.scalar_tensor_tensor(z2[:, one(t)], d4[t], gs_t[:, t : t + 1], inv[:, one(t)], MULT, MULT)
        z2_bf = sb.tile([P, ROW], BF16, name="z2_bf", tag="z2_bf", align_bytes=64)
        nc.vector.tensor_copy(
            z2_bf[:].rearrange("p (c t) -> p c t", t=PACK), z2[:].rearrange("p (t c) -> p c t", t=PACK)
        )
        z2_w = new("z2_w", S, U32)
        quantize(z2_w[:], z2_s[:], z2_bf[:])
        b_ps = product("db", 2, xc_wd, P, FP8X4, xc_sd, z2_w[:], z2_s[:])

        a5 = dsq[:, 3 * S : 3 * S + ROW]
        a6 = new("a6", ROW, F32)
        u = new("u", ROW, F32)
        v = new("v", ROW, F32)
        b = new("b", ROW, F32)
        for t in range(PACK):
            nc.scalar.activation(a5[:, one(t)], window(a, t).indirect(l_n5[:]), COPY)
        for t in range(PACK):
            nc.scalar.activation(a6[:, one(t)], window(a, t).indirect(l_n6[:]), COPY)
        e5 = [
            sb.tile([P, 2 * S], F32, name="e5_0", tag="z2_bf", align_bytes=64),
            sb.tile([P, 2 * S], F32, name="e5_1", tag="xc_wd", align_bytes=64),
        ]
        nc.vector.tensor_tensor(e5[0][:], a5[:, pair(0)], a_ps[0][:], SUB)
        for i in range(2):
            nc.vector.tensor_scalar(b[:, pair(i)], b_ps[i][:], 0.5 * 0.0625, None, MULT)
        nc.vector.tensor_tensor(e5[1][:], a5[:, pair(1)], a_ps[1][:], SUB)
        for i in range(2):
            nc.vector.scalar_tensor_tensor(u[:, pair(i)], b_ps[i][:], 0.0625, e5[i][:], MULT, MULT)
            nc.gpsimd.tensor_tensor(v[:, pair(i)], a6[:, pair(i)], a[:, pair(i)], SUB)

        b7 = new("b7", ROW, F32)
        res = new("res", ROW, F32)
        res_bf = new("res_bf", ROW, BF16)
        o_w = new("o_w", S, U32)
        by_t = lambda tile: tile[:].rearrange("p (t c) -> p t c", t=PACK)
        out_rows = out_0.rearrange("(p t) c -> p t c", t=PACK)
        for h in range(2):
            cols = slice(HALF * h, HALF * (h + 1))
            for t in range(PACK):
                nc.scalar.activation(
                    by_t(b7)[:, t, cols], b[:, one(t)].indirect(l_n7[:, HALF // 16 * h : HALF // 16 * (h + 1)]), COPY
                )
            step = 2
            for t in range(0, PACK, step):
                nc.vector.tensor_tensor(
                    by_t(b7)[:, t : t + step, cols], by_t(b7)[:, t : t + step, cols], by_t(v)[:, t : t + step, cols], MULT
                )
            for t in range(0, PACK, step):
                nc.vector.tensor_tensor(
                    by_t(res)[:, t : t + step, cols], by_t(b7)[:, t : t + step, cols], by_t(u)[:, t : t + step, cols], ADD
                )
            nc.sync.dma_start(out_rows[:, :, cols], by_t(res)[:, :, cols])
            grouped = res_bf[:, PACK * HALF * h : PACK * HALF * (h + 1)]
            nc.vector.tensor_copy(
                grouped.rearrange("p (c t) -> p c t", t=PACK), by_t(res)[:, :, cols].rearrange("p t c -> p c t")
            )
            quantize(o_w[:, cols], o_s[:, cols], grouped)
            (nc.sync if h == 0 else nc.scalar).dma_start(
                out_1[0].rearrange("p c r -> p (c r)").bitcast(I32)[:, cols], o_w[:, cols].bitcast(I32)
            )
        for q in range(4):
            queue = nc.sync if q % 2 == 0 else nc.scalar
            queue.dma_start(out_2[0, 4 * q : 4 * q + 4, :].bitcast(I32), o_s[32 * q : 32 * q + 4, :].bitcast(I32))
